import numpy as np
import ml_dtypes


def mxq(x, axis, fmt="e4m3"):
    dtype, down = {"e4m3": (ml_dtypes.float8_e4m3fn, 7), "e5m2": (ml_dtypes.float8_e5m2, 14)}[fmt]
    v = np.moveaxis(np.asarray(x, np.float32).astype(ml_dtypes.bfloat16).astype(np.float64), axis, -1)
    blocks = v.reshape(v.shape[:-1] + (-1, 32))
    amax = np.abs(blocks).max(-1, keepdims=True)
    byte = np.maximum(np.where(amax > 0, np.frexp(amax)[1] - 1 + 127, 0) - down, 1)
    scale = np.exp2(byte - 127.0)
    codes = (blocks / scale).astype(np.float32).astype(dtype).astype(np.float64)
    return np.moveaxis((codes * scale).reshape(v.shape), -1, axis)


WIDE = False


def mx_kscale(k):
    if not WIDE:
        return np.ones(k)
    levels = np.array([10, -10, 5, -5, 0])
    if k % 512:
        return np.exp2(np.random.permutation(np.resize(levels, k // 32))).repeat(32)
    a = np.empty((k // 512, 16))
    for p in range(k // 512):
        a[p, :8] = np.random.permutation(np.resize(levels, 8))
        for g in range(8):
            far = levels[np.abs(levels - a[p, g]) >= 10]
            a[p, g + 8] = far[np.random.randint(len(far))]
    return np.exp2(a.ravel()).repeat(32)


def f64(x):
    return np.asarray(x).astype(np.float64)


def striped(idx):
    return np.tile(idx.reshape(-1, 16).T, (8, 1)).astype(np.uint16)


def unstriped(offs):
    return offs[:16].T.reshape(-1).astype(np.int64)


def pack_weight(w):
    k, n = w.shape
    w = f64(np.asarray(w, np.float32).astype(ml_dtypes.bfloat16)).reshape(k // 32, 32, n)
    amax = np.abs(w).max(1)
    byte = np.clip(np.where(amax > 0, np.frexp(amax)[1] - 1 + 127 - 7, 1), 1, 254)
    scaled = (w * np.exp2(127.0 - byte)[:, None, :]).reshape(k, n).astype(np.float32)
    words = np.ascontiguousarray(scaled.reshape(k // 512, 128, 4, n).transpose(0, 1, 3, 2)).astype(ml_dtypes.float8_e4m3fn).view(np.uint8)
    return words, np.ascontiguousarray(byte.astype(np.uint8).reshape(k // 512, 16, n))


def unpack_weight(words, scales):
    g, p, n, _ = words.shape
    vals = np.ascontiguousarray(words).view(ml_dtypes.float8_e4m3fn).astype(np.float64) * np.repeat(np.exp2(scales.astype(np.float64) - 127.0), 8, axis=1)[..., None]
    return vals.transpose(0, 1, 3, 2).reshape(g * 512, n)


K, T, S, N, V = 512, 2048, 512, 256, 256


def setup_inputs():
    n = np.random.standard_normal
    s = mx_kscale(K)[:, None]
    packed_xT = pack_weight(n((K, T)) * s)
    return {
        "x_words": packed_xT[0],
        "x_scales": packed_xT[1],
        "w1": (n((K, N)) / np.sqrt(K) / s).astype(np.float32),
        "w2": (n((K, N)) / np.sqrt(K) / s).astype(np.float32),
        "gx": (n((N, V))).astype(np.float32),
        "gy": (n((N, V))).astype(np.float32),
        "gt": (n((N, V))).astype(np.float32),
        "reg": (np.random.uniform(0.5, 3.0, (N, 1))).astype(np.float32),
        "offs": striped(np.random.permutation(T)[:S]),
        "pos1": striped(np.random.permutation(S)[:V]),
        "pos2": striped(np.random.permutation(S)[:V]),
        "pos3": striped(np.random.permutation(S)[:V]),
        "pos4": striped(np.random.permutation(S)[:V]),
    }


def reference(x_words, x_scales, w1, w2, gx, gy, gt, reg, offs, pos1, pos2, pos3, pos4):
    xq = unpack_weight(x_words, x_scales)[:, unstriped(offs)]
    uo = mxq(f64(w1), 0, "e4m3").T @ xq
    ub = (uo[:, unstriped(pos1)] + uo[:, unstriped(pos2)] + uo[:, unstriped(pos3)] + uo[:, unstriped(pos4)]) / 4
    vo = mxq(f64(w2), 0, "e4m3").T @ xq
    vb = (vo[:, unstriped(pos1)] + vo[:, unstriped(pos2)] + vo[:, unstriped(pos3)] + vo[:, unstriped(pos4)]) / 4
    res = f64(gx) * ub + f64(gy) * vb + f64(gt)
    return ub - ((f64(gx) * res) / ((f64(gx)) ** 2 + (f64(gy)) ** 2 + f64(reg)))

@@ -1,0 +1,222 @@
+from contextlib import ExitStack
+
+import concourse.mybir as mybir
+from concourse.masks import make_identity
+
+K, T, S, M, V = 512, 2048, 512, 256, 256
+FLOPS = 2 * 2 * K * M * S
+
+F32 = mybir.dt.float32
+BF16 = mybir.dt.bfloat16
+I32 = mybir.dt.int32
+U32 = mybir.dt.uint32
+U16 = mybir.dt.uint16
+U8 = mybir.dt.uint8
+FP8X4 = mybir.dt.float8_e4m3fn_x4
+ACT = mybir.ActivationFunctionType
+ALU = mybir.AluOpType
+
+P = 128
+PACK = 4
+BLOCKS = M // P
+HALVES = V // P
+LISTS = 4
+S_HALF = S // 2
+
+
+def tile_picked_yhorn_quad_p_kernel(
+    tc, x_words, x_scales, w1, w2, gx, gy, gt, reg, offs, pos1, pos2, pos3, pos4, out
+):
+    nc = tc.nc
+    with ExitStack() as ctx:
+        keep = ctx.enter_context(tc.tile_pool(name="keep", bufs=1))
+        psum = ctx.enter_context(tc.psum_pool(name="psum", bufs=1))
+
+        def sb(name, shape, dtype):
+            return keep.tile(shape, dtype, name=name, align_bytes=64)
+
+        x_sc = sb("x_sc", [P, T], U8)
+        nc.gpsimd.memset(x_sc[:].bitcast(I32), 0)
+        one = sb("one", [P, 1], F32)
+        nc.vector.memset(one[:], 1.0)
+
+        offs_t = keep.tile([P, S // 16], U16, name="offs_t")
+        nc.sync.dma_start(offs_t[:], offs)
+        w1_raw = sb("w1_raw", [P, PACK, M], F32)
+        nc.sync.dma_start(w1_raw[:], w1.rearrange("(p j) m -> p j m", j=PACK))
+        for q in range(4):
+            nc.sync.dma_start(
+                x_sc[32 * q : 32 * q + 4, :].bitcast(I32), x_scales[0, 4 * q : 4 * q + 4, :].bitcast(I32)
+            )
+        x_w = sb("x_w", [P, T], I32)
+        nc.sync.dma_start(x_w[:], x_words[0].rearrange("p n t -> p (n t)").bitcast(I32))
+        warm = sb("warm", [P, 1], F32)
+        nc.scalar.activation(warm[:], one[:], ACT.Abs_reciprocal_sqrt)
+
+        g_t = {}
+        for name, src in (("gx", gx), ("gy", gy)):
+            g_t[name] = sb(name + "_t", [P, BLOCKS, V], F32)
+            nc.sync.dma_start(g_t[name][:], src.rearrange("(b p) v -> p b v", p=P))
+        pos_t = []
+        for i, pos in enumerate((pos1, pos2, pos3, pos4)):
+            pos_t.append(keep.tile([P, V // 16], U16, name="pos_t%d" % i))
+            nc.sync.dma_start(pos_t[i][:], pos)
+        g_t["gt"] = sb("gt_t", [P, BLOCKS, V], F32)
+        nc.sync.dma_start(g_t["gt"][:], gt.rearrange("(b p) v -> p b v", p=P))
+        reg_t = sb("reg_t", [P, BLOCKS, 1], F32)
+        with nc.allow_non_contiguous_dma(reason="one regularisation value a row"):
+            nc.sync.dma_start(reg_t[:], reg.rearrange("(b p) o -> p b o", p=P))
+        w2_raw = sb("w2_raw", [P, PACK, M], F32)
+        nc.sync.dma_start(w2_raw[:], w2.rearrange("(p j) m -> p j m", j=PACK))
+
+        ident = sb("ident", [P, P], F32)
+        make_identity(nc, ident[:])
+
+        def interleaved(grouped, raw):
+            return (
+                grouped.rearrange("p (c i) t -> p c t i", i=4),
+                raw.rearrange("p t (c i) -> p c t i", i=4),
+            )
+
+        w_grp = [sb("w_grp%d" % a, [P, M, PACK], BF16) for a in range(2)]
+        w_codes = [sb("w_codes%d" % a, [P, M], U32) for a in range(2)]
+        w_sc = [sb("w_sc%d" % a, [P, M], U8) for a in range(2)]
+
+        dst, src = interleaved(w_grp[0][:], w1_raw[:])
+        nc.vector.tensor_copy(dst, src)
+        xs = sb("xs", [P, S], U8)
+        nc.vector.tensor_copy(xs[:], x_sc[:].indirect(offs_t[:]))
+        nc.vector.quantize_mx(
+            out=w_codes[0][:].bitcast(FP8X4), scales=w_sc[0][:], in_=w_grp[0][:].rearrange("p c t -> p (c t)")
+        )
+        xw = sb("xw", [P, S], U32)
+        for c in range(2):
+            nc.vector.tensor_copy(
+                xw[:, c * S_HALF : (c + 1) * S_HALF],
+                x_w[:].bitcast(U32).indirect(offs_t[:, c * (S_HALF // 16) : (c + 1) * (S_HALF // 16)]),
+            )
+
+        flow = {(a, b): sb("flow%d%d" % (a, b), [P, S], F32) for a in range(2) for b in range(BLOCKS)}
+
+        def product(a, b, cols, bank):
+            rows = slice(b * P, (b + 1) * P)
+            acc = psum.tile([P, S], F32, name="acc", tag="acc%d" % bank)
+            width = cols.stop - cols.start
+            nc.tensor.matmul_mx(
+                out=acc[:, :width],
+                lhsT=w_codes[a][:, rows].bitcast(FP8X4),
+                lhsT_scale=w_sc[a][:, rows],
+                rhs=xw[:, cols].bitcast(FP8X4),
+                rhs_scale=xs[:, cols],
+                start=True,
+                stop=True,
+            )
+            nc.scalar.activation(flow[a, b][:, cols], acc[:, :width], ACT.Copy, scale=1.0 / LISTS)
+
+        product(0, 0, slice(0, S_HALF), 0)
+        product(0, 0, slice(S_HALF, S), 1)
+        product(0, 1, slice(0, S), 0)
+
+        def flat(t):
+            return t[:].rearrange("p b v -> p (b v)")
+
+        xy = sb("xy", [P, BLOCKS, V], F32)
+        nc.vector.tensor_tensor(flat(xy), flat(g_t["gx"]), flat(g_t["gy"]), ALU.mult)
+        xt = sb("xt", [P, BLOCKS, V], F32)
+        nc.vector.tensor_tensor(flat(xt), flat(g_t["gx"]), flat(g_t["gt"]), ALU.mult)
+
+        def turned(name, t, scale, bank):
+            ps = psum.tile([P, BLOCKS, HALVES, P], F32, name="turn", tag="turn%d" % bank)
+            for b in range(BLOCKS):
+                for h in range(HALVES):
+                    nc.tensor.transpose(ps[:, b, h, :], t[:, b, h * P : (h + 1) * P], ident[:])
+            res = sb(name, [P, BLOCKS, HALVES, P], F32)
+            nc.scalar.activation(
+                res[:].rearrange("p b h m -> p (b h m)"), ps[:].rearrange("p b h m -> p (b h m)"), ACT.Copy, scale=scale
+            )
+            return res
+
+        def mean_turned(a, b, bank):
+            ps = psum.tile([P, HALVES, P], F32, name="mean", tag="mean%d" % bank)
+            for i in range(LISTS):
+                picked = sb("picked%d%d%d" % (a, b, i), [P, V], F32)
+                nc.vector.tensor_copy(picked[:], flow[a, b][:].indirect(pos_t[i][:]))
+                for h in range(HALVES):
+                    nc.tensor.matmul(
+                        ps[:, h, :], picked[:, h * P : (h + 1) * P], ident[:], is_transpose=True,
+                        start=(i == 0 and h == 0), stop=(i == LISTS - 1 and h == HALVES - 1),
+                    )
+            return ps
+
+        def weighted(name, mean, factor, b):
+            term = sb(name, [P, HALVES, P], F32)
+            nc.vector.tensor_tensor(
+                term[:].rearrange("p h m -> p (h m)"), mean[:].rearrange("p h m -> p (h m)"),
+                factor[:, b].rearrange("p h m -> p (h m)"), ALU.mult,
+            )
+            return term
+
+        def add_back(ps, term, start, stop):
+            for h in range(HALVES):
+                nc.tensor.matmul(
+                    ps[:, h, :], term[:, h, :], ident[:], is_transpose=True,
+                    start=(start and h == 0), stop=(stop and h == HALVES - 1),
+                )
+
+        def quantise_w2(b):
+            rows = slice(b * P, (b + 1) * P)
+            nc.vector.quantize_mx(
+                out=w_codes[1][:, rows].bitcast(FP8X4), scales=w_sc[1][:, rows],
+                in_=w_grp[1][:, rows, :].rearrange("p c t -> p (c t)"),
+            )
+
+        def cast_w2(b):
+            rows = slice(b * P, (b + 1) * P)
+            dst2, src2 = interleaved(w_grp[1][:, rows, :], w2_raw[:, :, rows])
+            nc.scalar.copy(dst2, src2)
+
+        sqy = sb("sqy", [P, BLOCKS, V], F32)
+        nc.scalar.activation(flat(sqy), flat(g_t["gy"]), ACT.Square)
+        rest = sb("rest", [P, BLOCKS, V], F32)
+        for b in range(BLOCKS):
+            nc.scalar.activation(rest[:, b, :], sqy[:, b, :], ACT.Identity, bias=reg_t[:, b, :])
+        cast_w2(0)
+
+        mean_u0 = mean_turned(0, 0, 0)
+        rest_T = turned("rest_T", rest, 1.0, 0)
+        quantise_w2(0)
+        product(1, 0, slice(0, S), 1)
+        cast_w2(1)
+        xy_T = turned("xy_T", xy, -1.0, 1)
+        mean_u1 = mean_turned(0, 1, 1)
+        quantise_w2(1)
+        product(1, 1, slice(0, S), 0)
+        sqx = sb("sqx", [P, BLOCKS, V], F32)
+        nc.scalar.activation(flat(sqx), flat(g_t["gx"]), ACT.Square)
+        xt_T = turned("xt_T", xt, -1.0, 0)
+        term_u = [weighted("term_u0", mean_u0, rest_T, 0)]
+        num = [psum.tile([P, HALVES, P], F32, name="num%d" % b) for b in range(BLOCKS)]
+        add_back(num[0], term_u[0], True, False)
+
+        mean_v0 = mean_turned(1, 0, 0)
+        term_u.append(weighted("term_u1", mean_u1, rest_T, 1))
+        add_back(num[1], term_u[1], True, False)
+        den = sb("den", [P, BLOCKS, V], F32)
+        nc.vector.tensor_tensor(flat(den), flat(sqx), flat(rest), ALU.add)
+        root = sb("root", [P, BLOCKS, V], F32)
+        nc.scalar.activation(flat(root), flat(den), ACT.Abs_reciprocal_sqrt)
+        inv = sb("inv", [P, BLOCKS, V], F32)
+        nc.scalar.activation(flat(inv), flat(root), ACT.Square)
+        for b in range(BLOCKS):
+            add_back(num[b], xt_T[:, b], False, False)
+
+        def finish(b, mean_v):
+            term_v = weighted("term_v%d" % b, mean_v, xy_T, b)
+            add_back(num[b], term_v, False, True)
+            res = sb("res%d" % b, [P, V], F32)
+            nc.vector.tensor_tensor(res[:], num[b][:].rearrange("p h v -> p (h v)"), inv[:, b, :], ALU.mult)
+            nc.sync.dma_start(out[b * P : (b + 1) * P, :], res[:])
+
+        mean_v1 = mean_turned(1, 1, 1)
+        finish(0, mean_v0)
+        finish(1, mean_v1)

@@ -32,42 +32,41 @@ def tile_picked_yhorn_quad_p_kernel(
         keep = ctx.enter_context(tc.tile_pool(name="keep", bufs=1))
         psum = ctx.enter_context(tc.psum_pool(name="psum", bufs=1))
 
-        def sb(name, shape, dtype):
-            return keep.tile(shape, dtype, name=name, align_bytes=64)
+        def sb(name, shape, dtype, tag=None):
+            return keep.tile(shape, dtype, name=name, tag=tag or name, align_bytes=64)
 
         x_sc = sb("x_sc", [P, T], U8)
         nc.gpsimd.memset(x_sc[:].bitcast(I32), 0)
         one = sb("one", [P, 1], F32)
         nc.vector.memset(one[:], 1.0)
 
-        offs_t = keep.tile([P, S // 16], U16, name="offs_t")
-        nc.sync.dma_start(offs_t[:], offs)
-        w1_raw = sb("w1_raw", [P, PACK, M], F32)
-        nc.sync.dma_start(w1_raw[:], w1.rearrange("(p j) m -> p j m", j=PACK))
+        w1_rows = w1.rearrange("(p j) m -> p j m", j=PACK)
+        w1_raw = [sb("w1_raw%d" % b, [P, PACK, P], F32) for b in range(BLOCKS)]
+        nc.sync.dma_start(w1_raw[0][:], w1_rows[:, :, 0:P])
         for q in range(4):
             nc.sync.dma_start(
                 x_sc[32 * q : 32 * q + 4, :].bitcast(I32), x_scales[0, 4 * q : 4 * q + 4, :].bitcast(I32)
             )
+        offs_t = keep.tile([P, S // 16], U16, name="offs_t")
+        nc.sync.dma_start(offs_t[:], offs)
         x_w = sb("x_w", [P, T], I32)
         nc.sync.dma_start(x_w[:], x_words[0].rearrange("p n t -> p (n t)").bitcast(I32))
+        pos_t = [keep.tile([P, V // 16], U16, name="pos_t%d" % i) for i in range(LISTS)]
+        for i, pos in enumerate((pos1, pos2, pos3)):
+            nc.sync.dma_start(pos_t[i][:], pos)
+        nc.sync.dma_start(w1_raw[1][:], w1_rows[:, :, P : 2 * P])
+        w2_raw = sb("w2_raw", [P, PACK, M], F32)
+        nc.sync.dma_start(w2_raw[:], w2.rearrange("(p j) m -> p j m", j=PACK))
+        nc.sync.dma_start(pos_t[3][:], pos4)
         warm = sb("warm", [P, 1], F32)
         nc.scalar.activation(warm[:], one[:], ACT.Abs_reciprocal_sqrt)
-
-        g_t = {}
-        for name, src in (("gx", gx), ("gy", gy)):
-            g_t[name] = sb(name + "_t", [P, BLOCKS, V], F32)
-            nc.sync.dma_start(g_t[name][:], src.rearrange("(b p) v -> p b v", p=P))
-        pos_t = []
-        for i, pos in enumerate((pos1, pos2, pos3, pos4)):
-            pos_t.append(keep.tile([P, V // 16], U16, name="pos_t%d" % i))
-            nc.sync.dma_start(pos_t[i][:], pos)
-        g_t["gt"] = sb("gt_t", [P, BLOCKS, V], F32)
-        nc.sync.dma_start(g_t["gt"][:], gt.rearrange("(b p) v -> p b v", p=P))
         reg_t = sb("reg_t", [P, BLOCKS, 1], F32)
         with nc.allow_non_contiguous_dma(reason="one regularisation value a row"):
             nc.sync.dma_start(reg_t[:], reg.rearrange("(b p) o -> p b o", p=P))
-        w2_raw = sb("w2_raw", [P, PACK, M], F32)
-        nc.sync.dma_start(w2_raw[:], w2.rearrange("(p j) m -> p j m", j=PACK))
+        g_t = {}
+        for name, src in (("gy", gy), ("gx", gx), ("gt", gt)):
+            g_t[name] = sb(name + "_t", [P, BLOCKS, V], F32)
+            nc.sync.dma_start(g_t[name][:], src.rearrange("(b p) v -> p b v", p=P))
 
         ident = sb("ident", [P, P], F32)
         make_identity(nc, ident[:])
@@ -78,17 +77,25 @@ def tile_picked_yhorn_quad_p_kernel(
                 raw.rearrange("p t (c i) -> p c t i", i=4),
             )
 
-        w_grp = [sb("w_grp%d" % a, [P, M, PACK], BF16) for a in range(2)]
+        w_grp = {(a, b): sb("w_grp%d%d" % (a, b), [P, P, PACK], BF16) for a in range(2) for b in range(BLOCKS)}
         w_codes = [sb("w_codes%d" % a, [P, M], U32) for a in range(2)]
         w_sc = [sb("w_sc%d" % a, [P, M], U8) for a in range(2)]
 
-        dst, src = interleaved(w_grp[0][:], w1_raw[:])
-        nc.vector.tensor_copy(dst, src)
+        def quantise(a, b):
+            rows = slice(b * P, (b + 1) * P)
+            nc.vector.quantize_mx(
+                out=w_codes[a][:, rows].bitcast(FP8X4), scales=w_sc[a][:, rows],
+                in_=w_grp[a, b][:].rearrange("p c t -> p (c t)"),
+            )
+
+        def cast_w1(b):
+            dst, src = interleaved(w_grp[0, b][:], w1_raw[b][:])
+            nc.vector.tensor_copy(dst, src)
+
+        cast_w1(0)
         xs = sb("xs", [P, S], U8)
         nc.vector.tensor_copy(xs[:], x_sc[:].indirect(offs_t[:]))
-        nc.vector.quantize_mx(
-            out=w_codes[0][:].bitcast(FP8X4), scales=w_sc[0][:], in_=w_grp[0][:].rearrange("p c t -> p (c t)")
-        )
+        quantise(0, 0)
         xw = sb("xw", [P, S], U32)
         for c in range(2):
             nc.vector.tensor_copy(
@@ -115,18 +122,20 @@ def tile_picked_yhorn_quad_p_kernel(
 
         product(0, 0, slice(0, S_HALF), 0)
         product(0, 0, slice(S_HALF, S), 1)
+        cast_w1(1)
+        quantise(0, 1)
         product(0, 1, slice(0, S), 0)
 
         def flat(t):
             return t[:].rearrange("p b v -> p (b v)")
 
         xy = sb("xy", [P, BLOCKS, V], F32)
-        nc.vector.tensor_tensor(flat(xy), flat(g_t["gx"]), flat(g_t["gy"]), ALU.mult)
+        nc.gpsimd.tensor_tensor(flat(xy), flat(g_t["gx"]), flat(g_t["gy"]), ALU.mult)
         xt = sb("xt", [P, BLOCKS, V], F32)
-        nc.vector.tensor_tensor(flat(xt), flat(g_t["gx"]), flat(g_t["gt"]), ALU.mult)
+        nc.gpsimd.tensor_tensor(flat(xt), flat(g_t["gx"]), flat(g_t["gt"]), ALU.mult)
 
         def turned(name, t, scale, bank):
-            ps = psum.tile([P, BLOCKS, HALVES, P], F32, name="turn", tag="turn%d" % bank)
+            ps = psum.tile([P, BLOCKS, HALVES, P], F32, name="turn", tag=bank)
             for b in range(BLOCKS):
                 for h in range(HALVES):
                     nc.tensor.transpose(ps[:, b, h, :], t[:, b, h * P : (h + 1) * P], ident[:])
@@ -136,20 +145,20 @@ def tile_picked_yhorn_quad_p_kernel(
             )
             return res
 
-        def mean_turned(a, b, bank):
-            ps = psum.tile([P, HALVES, P], F32, name="mean", tag="mean%d" % bank)
+        def mean_turned(a, b, bank, after=None):
+            ps = psum.tile([P, HALVES, P], F32, name="mean", tag=bank)
+            picked = sb("picked%d%d" % (a, b), [P, LISTS, V], F32, tag=after)
             for i in range(LISTS):
-                picked = sb("picked%d%d%d" % (a, b, i), [P, V], F32)
-                nc.vector.tensor_copy(picked[:], flow[a, b][:].indirect(pos_t[i][:]))
+                nc.vector.tensor_copy(picked[:, i, :], flow[a, b][:].indirect(pos_t[i][:]))
                 for h in range(HALVES):
                     nc.tensor.matmul(
-                        ps[:, h, :], picked[:, h * P : (h + 1) * P], ident[:], is_transpose=True,
+                        ps[:, h, :], picked[:, i, h * P : (h + 1) * P], ident[:], is_transpose=True,
                         start=(i == 0 and h == 0), stop=(i == LISTS - 1 and h == HALVES - 1),
                     )
             return ps
 
-        def weighted(name, mean, factor, b):
-            term = sb(name, [P, HALVES, P], F32)
+        def weighted(name, mean, factor, b, after=None):
+            term = sb(name, [P, HALVES, P], F32, tag=after)
             nc.vector.tensor_tensor(
                 term[:].rearrange("p h m -> p (h m)"), mean[:].rearrange("p h m -> p (h m)"),
                 factor[:, b].rearrange("p h m -> p (h m)"), ALU.mult,
@@ -163,60 +172,49 @@ def tile_picked_yhorn_quad_p_kernel(
                     start=(start and h == 0), stop=(stop and h == HALVES - 1),
                 )
 
-        def quantise_w2(b):
-            rows = slice(b * P, (b + 1) * P)
-            nc.vector.quantize_mx(
-                out=w_codes[1][:, rows].bitcast(FP8X4), scales=w_sc[1][:, rows],
-                in_=w_grp[1][:, rows, :].rearrange("p c t -> p (c t)"),
-            )
-
         def cast_w2(b):
             rows = slice(b * P, (b + 1) * P)
-            dst2, src2 = interleaved(w_grp[1][:, rows, :], w2_raw[:, :, rows])
+            dst2, src2 = interleaved(w_grp[1, b][:], w2_raw[:, :, rows])
             nc.scalar.copy(dst2, src2)
+
+        cast_w2(0)
+        cast_w2(1)
+        mean_u0 = mean_turned(0, 0, "mean_u0", after="w_grp01")
+        quantise(1, 0)
+        quantise(1, 1)
+        product(1, 0, slice(0, S), 1)
+        product(1, 1, slice(0, S), 0)
 
         sqy = sb("sqy", [P, BLOCKS, V], F32)
         nc.scalar.activation(flat(sqy), flat(g_t["gy"]), ACT.Square)
         rest = sb("rest", [P, BLOCKS, V], F32)
         for b in range(BLOCKS):
             nc.scalar.activation(rest[:, b, :], sqy[:, b, :], ACT.Identity, bias=reg_t[:, b, :])
-        cast_w2(0)
-
-        mean_u0 = mean_turned(0, 0, 0)
-        rest_T = turned("rest_T", rest, 1.0, 0)
-        quantise_w2(0)
-        product(1, 0, slice(0, S), 1)
-        cast_w2(1)
-        xy_T = turned("xy_T", xy, -1.0, 1)
-        mean_u1 = mean_turned(0, 1, 1)
-        quantise_w2(1)
-        product(1, 1, slice(0, S), 0)
         sqx = sb("sqx", [P, BLOCKS, V], F32)
         nc.scalar.activation(flat(sqx), flat(g_t["gx"]), ACT.Square)
-        xt_T = turned("xt_T", xt, -1.0, 0)
-        term_u = [weighted("term_u0", mean_u0, rest_T, 0)]
-        num = [psum.tile([P, HALVES, P], F32, name="num%d" % b) for b in range(BLOCKS)]
-        add_back(num[0], term_u[0], True, False)
-
-        mean_v0 = mean_turned(1, 0, 0)
-        term_u.append(weighted("term_u1", mean_u1, rest_T, 1))
-        add_back(num[1], term_u[1], True, False)
         den = sb("den", [P, BLOCKS, V], F32)
-        nc.vector.tensor_tensor(flat(den), flat(sqx), flat(rest), ALU.add)
+        nc.gpsimd.tensor_tensor(flat(den), flat(sqx), flat(rest), ALU.add)
+        mean_u1 = mean_turned(0, 1, "mean_u1", after="w_grp11")
+        rest_T = turned("rest_T", rest, 1.0, "mean_v0")
+        xt_T = turned("xt_T", xt, -1.0, "acc1")
+        xy_T = turned("xy_T", xy, -1.0, "mean_v1")
         root = sb("root", [P, BLOCKS, V], F32)
         nc.scalar.activation(flat(root), flat(den), ACT.Abs_reciprocal_sqrt)
         inv = sb("inv", [P, BLOCKS, V], F32)
         nc.scalar.activation(flat(inv), flat(root), ACT.Square)
+        num = [psum.tile([P, HALVES, P], F32, name="num%d" % b) for b in range(BLOCKS)]
         for b in range(BLOCKS):
-            add_back(num[b], xt_T[:, b], False, False)
+            add_back(num[b], xt_T[:, b], True, False)
 
-        def finish(b, mean_v):
-            term_v = weighted("term_v%d" % b, mean_v, xy_T, b)
-            add_back(num[b], term_v, False, True)
+        mean_v0 = mean_turned(1, 0, "mean_v0")
+        for b, mean_u in enumerate((mean_u0, mean_u1)):
+            add_back(num[b], weighted("term_u%d" % b, mean_u, rest_T, b), False, False)
+
+        mean_v1 = mean_turned(1, 1, "mean_v1", after="rest_T")
+        terms_v = [weighted("term_v0", mean_v0, xy_T, 0), weighted("term_v1", mean_v1, xy_T, 1)]
+        for b in range(BLOCKS):
+            add_back(num[b], terms_v[b], False, True)
+        for b in range(BLOCKS):
             res = sb("res%d" % b, [P, V], F32)
             nc.vector.tensor_tensor(res[:], num[b][:].rearrange("p h v -> p (h v)"), inv[:, b, :], ALU.mult)
             nc.sync.dma_start(out[b * P : (b + 1) * P, :], res[:])
-
-        mean_v1 = mean_turned(1, 1, 1)
-        finish(0, mean_v0)
-        finish(1, mean_v1)

from contextlib import ExitStack

import concourse.mybir as mybir
from concourse.masks import make_identity

K, T, S, M, V = 512, 2048, 512, 256, 256
FLOPS = 2 * 2 * K * M * S

F32 = mybir.dt.float32
BF16 = mybir.dt.bfloat16
I32 = mybir.dt.int32
U32 = mybir.dt.uint32
U16 = mybir.dt.uint16
U8 = mybir.dt.uint8
FP8X4 = mybir.dt.float8_e4m3fn_x4
ACT = mybir.ActivationFunctionType
ALU = mybir.AluOpType

P = 128
PACK = 4
BLOCKS = M // P
HALVES = V // P
LISTS = 4
S_HALF = S // 2


def tile_picked_yhorn_quad_p_kernel(
    tc, x_words, x_scales, w1, w2, gx, gy, gt, reg, offs, pos1, pos2, pos3, pos4, out
):
    nc = tc.nc
    with ExitStack() as ctx:
        keep = ctx.enter_context(tc.tile_pool(name="keep", bufs=1))
        psum = ctx.enter_context(tc.psum_pool(name="psum", bufs=1))

        def sb(name, shape, dtype, tag=None):
            return keep.tile(shape, dtype, name=name, tag=tag or name, align_bytes=64)

        x_sc = sb("x_sc", [P, T], U8)
        nc.gpsimd.memset(x_sc[:].bitcast(I32), 0)
        one = sb("one", [P, 1], F32)
        nc.vector.memset(one[:], 1.0)

        w1_rows = w1.rearrange("(p j) m -> p j m", j=PACK)
        w1_raw = [sb("w1_raw%d" % b, [P, PACK, P], F32) for b in range(BLOCKS)]
        nc.sync.dma_start(w1_raw[0][:], w1_rows[:, :, 0:P])
        for q in range(4):
            nc.sync.dma_start(
                x_sc[32 * q : 32 * q + 4, :].bitcast(I32), x_scales[0, 4 * q : 4 * q + 4, :].bitcast(I32)
            )
        offs_t = keep.tile([P, S // 16], U16, name="offs_t")
        nc.sync.dma_start(offs_t[:], offs)
        x_w = sb("x_w", [P, T], I32)
        nc.sync.dma_start(x_w[:], x_words[0].rearrange("p n t -> p (n t)").bitcast(I32))
        pos_t = [keep.tile([P, V // 16], U16, name="pos_t%d" % i) for i in range(LISTS)]
        for i, pos in enumerate((pos1, pos2, pos3)):
            nc.sync.dma_start(pos_t[i][:], pos)
        nc.sync.dma_start(w1_raw[1][:], w1_rows[:, :, P : 2 * P])
        w2_raw = sb("w2_raw", [P, PACK, M], F32)
        nc.sync.dma_start(w2_raw[:], w2.rearrange("(p j) m -> p j m", j=PACK))
        nc.sync.dma_start(pos_t[3][:], pos4)
        warm = sb("warm", [P, 1], F32)
        nc.scalar.activation(warm[:], one[:], ACT.Abs_reciprocal_sqrt)
        reg_t = sb("reg_t", [P, BLOCKS, 1], F32)
        with nc.allow_non_contiguous_dma(reason="one regularisation value a row"):
            nc.sync.dma_start(reg_t[:], reg.rearrange("(b p) o -> p b o", p=P))
        g_t = {}
        for name, src in (("gy", gy), ("gx", gx), ("gt", gt)):
            g_t[name] = sb(name + "_t", [P, BLOCKS, V], F32)
            nc.sync.dma_start(g_t[name][:], src.rearrange("(b p) v -> p b v", p=P))

        ident = sb("ident", [P, P], F32)
        make_identity(nc, ident[:])

        def interleaved(grouped, raw):
            return (
                grouped.rearrange("p (c i) t -> p c t i", i=4),
                raw.rearrange("p t (c i) -> p c t i", i=4),
            )

        w_grp = {(a, b): sb("w_grp%d%d" % (a, b), [P, P, PACK], BF16) for a in range(2) for b in range(BLOCKS)}
        w_codes = [sb("w_codes%d" % a, [P, M], U32) for a in range(2)]
        w_sc = [sb("w_sc%d" % a, [P, M], U8) for a in range(2)]

        def quantise(a, b):
            rows = slice(b * P, (b + 1) * P)
            nc.vector.quantize_mx(
                out=w_codes[a][:, rows].bitcast(FP8X4), scales=w_sc[a][:, rows],
                in_=w_grp[a, b][:].rearrange("p c t -> p (c t)"),
            )

        def cast_w1(b):
            dst, src = interleaved(w_grp[0, b][:], w1_raw[b][:])
            nc.vector.tensor_copy(dst, src)

        cast_w1(0)
        xs = sb("xs", [P, S], U8)
        nc.vector.tensor_copy(xs[:], x_sc[:].indirect(offs_t[:]))
        quantise(0, 0)
        xw = sb("xw", [P, S], U32)
        for c in range(2):
            nc.vector.tensor_copy(
                xw[:, c * S_HALF : (c + 1) * S_HALF],
                x_w[:].bitcast(U32).indirect(offs_t[:, c * (S_HALF // 16) : (c + 1) * (S_HALF // 16)]),
            )

        flow = {(a, b): sb("flow%d%d" % (a, b), [P, S], F32) for a in range(2) for b in range(BLOCKS)}

        def product(a, b, cols, bank):
            rows = slice(b * P, (b + 1) * P)
            acc = psum.tile([P, S], F32, name="acc", tag="acc%d" % bank)
            width = cols.stop - cols.start
            nc.tensor.matmul_mx(
                out=acc[:, :width],
                lhsT=w_codes[a][:, rows].bitcast(FP8X4),
                lhsT_scale=w_sc[a][:, rows],
                rhs=xw[:, cols].bitcast(FP8X4),
                rhs_scale=xs[:, cols],
                start=True,
                stop=True,
            )
            nc.scalar.activation(flow[a, b][:, cols], acc[:, :width], ACT.Copy, scale=1.0 / LISTS)

        product(0, 0, slice(0, S_HALF), 0)
        product(0, 0, slice(S_HALF, S), 1)
        cast_w1(1)
        quantise(0, 1)
        product(0, 1, slice(0, S), 0)

        def flat(t):
            return t[:].rearrange("p b v -> p (b v)")

        xy = sb("xy", [P, BLOCKS, V], F32)
        nc.gpsimd.tensor_tensor(flat(xy), flat(g_t["gx"]), flat(g_t["gy"]), ALU.mult)
        xt = sb("xt", [P, BLOCKS, V], F32)
        nc.gpsimd.tensor_tensor(flat(xt), flat(g_t["gx"]), flat(g_t["gt"]), ALU.mult)

        def turned(name, t, scale, bank):
            ps = psum.tile([P, BLOCKS, HALVES, P], F32, name="turn", tag=bank)
            for b in range(BLOCKS):
                for h in range(HALVES):
                    nc.tensor.transpose(ps[:, b, h, :], t[:, b, h * P : (h + 1) * P], ident[:])
            res = sb(name, [P, BLOCKS, HALVES, P], F32)
            nc.scalar.activation(
                res[:].rearrange("p b h m -> p (b h m)"), ps[:].rearrange("p b h m -> p (b h m)"), ACT.Copy, scale=scale
            )
            return res

        def mean_turned(a, b, bank, after=None):
            ps = psum.tile([P, HALVES, P], F32, name="mean", tag=bank)
            picked = sb("picked%d%d" % (a, b), [P, LISTS, V], F32, tag=after)
            for i in range(LISTS):
                nc.vector.tensor_copy(picked[:, i, :], flow[a, b][:].indirect(pos_t[i][:]))
                for h in range(HALVES):
                    nc.tensor.matmul(
                        ps[:, h, :], picked[:, i, h * P : (h + 1) * P], ident[:], is_transpose=True,
                        start=(i == 0 and h == 0), stop=(i == LISTS - 1 and h == HALVES - 1),
                    )
            return ps

        def weighted(name, mean, factor, b, after=None):
            term = sb(name, [P, HALVES, P], F32, tag=after)
            nc.vector.tensor_tensor(
                term[:].rearrange("p h m -> p (h m)"), mean[:].rearrange("p h m -> p (h m)"),
                factor[:, b].rearrange("p h m -> p (h m)"), ALU.mult,
            )
            return term

        def add_back(ps, term, start, stop):
            for h in range(HALVES):
                nc.tensor.matmul(
                    ps[:, h, :], term[:, h, :], ident[:], is_transpose=True,
                    start=(start and h == 0), stop=(stop and h == HALVES - 1),
                )

        def cast_w2(b):
            rows = slice(b * P, (b + 1) * P)
            dst2, src2 = interleaved(w_grp[1, b][:], w2_raw[:, :, rows])
            nc.scalar.copy(dst2, src2)

        cast_w2(0)
        cast_w2(1)
        mean_u0 = mean_turned(0, 0, "mean_u0", after="w_grp01")
        quantise(1, 0)
        quantise(1, 1)
        product(1, 0, slice(0, S), 1)
        product(1, 1, slice(0, S), 0)

        sqy = sb("sqy", [P, BLOCKS, V], F32)
        nc.scalar.activation(flat(sqy), flat(g_t["gy"]), ACT.Square)
        rest = sb("rest", [P, BLOCKS, V], F32)
        for b in range(BLOCKS):
            nc.scalar.activation(rest[:, b, :], sqy[:, b, :], ACT.Identity, bias=reg_t[:, b, :])
        sqx = sb("sqx", [P, BLOCKS, V], F32)
        nc.scalar.activation(flat(sqx), flat(g_t["gx"]), ACT.Square)
        den = sb("den", [P, BLOCKS, V], F32)
        nc.gpsimd.tensor_tensor(flat(den), flat(sqx), flat(rest), ALU.add)
        mean_u1 = mean_turned(0, 1, "mean_u1", after="w_grp11")
        rest_T = turned("rest_T", rest, 1.0, "mean_v0")
        xt_T = turned("xt_T", xt, -1.0, "acc1")
        xy_T = turned("xy_T", xy, -1.0, "mean_v1")
        root = sb("root", [P, BLOCKS, V], F32)
        nc.scalar.activation(flat(root), flat(den), ACT.Abs_reciprocal_sqrt)
        inv = sb("inv", [P, BLOCKS, V], F32)
        nc.scalar.activation(flat(inv), flat(root), ACT.Square)
        num = [psum.tile([P, HALVES, P], F32, name="num%d" % b) for b in range(BLOCKS)]
        for b in range(BLOCKS):
            add_back(num[b], xt_T[:, b], True, False)

        mean_v0 = mean_turned(1, 0, "mean_v0")
        for b, mean_u in enumerate((mean_u0, mean_u1)):
            add_back(num[b], weighted("term_u%d" % b, mean_u, rest_T, b), False, False)

        mean_v1 = mean_turned(1, 1, "mean_v1", after="rest_T")
        terms_v = [weighted("term_v0", mean_v0, xy_T, 0), weighted("term_v1", mean_v1, xy_T, 1)]
        for b in range(BLOCKS):
            add_back(num[b], terms_v[b], False, True)
        for b in range(BLOCKS):
            res = sb("res%d" % b, [P, V], F32)
            nc.vector.tensor_tensor(res[:], num[b][:].rearrange("p h v -> p (h v)"), inv[:, b, :], ALU.mult)
            nc.sync.dma_start(out[b * P : (b + 1) * P, :], res[:])
